import numpy as np, ml_dtypes
CORES = [2,34,66,98,130,162,194,226,258,290,322,354,386,418,450,482]
N = 16
KB, QP = 1, 256
WB = 3
def setup_inputs(rng):
    q = rng.standard_normal((N, 128, QP), dtype=np.float32) / 4; k = rng.standard_normal((N, 128, KB * 128), dtype=np.float32)
    a = 2 * np.pi * rng.random((N, QP)); s = 400 * rng.random((N, QP)) ** 1.5; q[:, 0, :] = s * np.cos(a); q[:, 1, :] = s * np.sin(a); q[:, 2, :] = 150 * rng.standard_normal((N, QP)); k[:, 2, :] = 1 + k[:, 2, :] / 50
    a = (2 * np.pi * rng.random() + np.pi / 2 * (rng.permutation(N).reshape(N, 1, 1) + 0.5) / N - 0.5 + (np.arange(KB).reshape(1, KB, 1) + rng.random((N, KB, 128))) / KB).reshape(N, KB * 128); k[:, 0, :] = np.cos(a); k[:, 1, :] = np.sin(a)
    return {"q": q.astype(ml_dtypes.bfloat16), "k": k.astype(ml_dtypes.bfloat16), "v": rng.standard_normal((N, 128, KB * 128), dtype=np.float32).astype(ml_dtypes.bfloat16)}
def setup_inputs_big(rng):
    d = setup_inputs(rng)
    for k in ("v",): d[k] = (d[k].astype(np.float32) * 1048576.0).astype(d[k].dtype)
    return d
def setup_inputs_small(rng):
    d = setup_inputs(rng)
    for k in ("v",): d[k] = (d[k].astype(np.float32) * (1 / 1048576.0)).astype(d[k].dtype)
    return d
def reference(q, k, v):
    Q, K, V = q.astype(np.float64), k.astype(np.float64), v.astype(np.float64)
    y = np.zeros((N, QP, 128))
    for r in range(N):
        js = list(range(max(0, r - WB), r + 1))
        S = np.concatenate([K[j].T @ Q[r] for j in js], axis=0)
        P = np.exp(S - S.max(axis=0)); P = P / P.sum(axis=0)
        y[r] = P.T @ np.concatenate([V[j][:, 128 * b:128 * b + 128] for j in js for b in range(KB)], axis=0)
    return {"y": y.astype(ml_dtypes.bfloat16)}

@@ -1,0 +1,278 @@
+from concourse.bass import DstId, RemoteDMATransfer
+from concourse.mybir import AluOpType, ActivationFunctionType
+
+WB = 3
+NS = WB + 1
+SW = 264
+SPLIT = True
+RELAY_MIN = 2
+NENG = 8
+
+SCRATCH = {
+    "kv": ("sbuf", [128, NS * SW], "bfloat16"),
+    "qs": ("sbuf", [128, 256], "bfloat16"),
+    "qd": ("sbuf", [128, 256], "bfloat16"),
+    "ones": ("sbuf", [128, 128], "bfloat16"),
+    "zero": ("sbuf", [128, 128], "bfloat16"),
+    "ident": ("sbuf", [128, 128], "bfloat16"),
+    "scr": ("sbuf", [128, 2 * NS * 128], "bfloat16"),
+    "dg": ("sbuf", [128, 512], "bfloat16"),
+    "pw": ("sbuf", [128, NS * 256], "bfloat16"),
+    "ze": ("sbuf", [128, 2 * 136], "bfloat16"),
+    "ce": ("sbuf", [128, 4], "float32"),
+    "rec": ("sbuf", [128, 4], "float32"),
+    "ysb": ("sbuf", [128, 256], "bfloat16"),
+}
+for _i in range(8):
+    SCRATCH["ps%d" % _i] = ("psum", [128, 512], "float32")
+
+SEMAPHORES = (["kld", "vld", "qld", "m1", "m2", "m3", "idn", "vq", "de", "dd", "oe", "ce", "ze", "ls", "rc",
+               "os0", "os1", "ys", "st", "snd"]
+              + ["ks%d" % s for s in range(NS)] + ["vs%d" % s for s in range(NS)]
+              + ["sa%d%d" % (b, t) for b in range(NS) for t in range(2)]
+              + ["sc%d%d" % (b, t) for b in range(NS) for t in range(2)]
+              + ["sb%d" % b for b in range(NS)] + ["p%d" % b for b in range(NS)])
+
+
+def _engines(mask, n):
+    out, c, b = 0, 0, 1
+    while c < n:
+        if mask & b:
+            out |= b
+            c += 1
+        b <<= 1
+    return out
+
+
+def _plan(T, topo):
+    cores = list(T.cores)
+    n = len(cores)
+    world = (max(topo.host(c) for c in cores) + 1) * topo.CORES_PER_HOST
+    plan, nrel = [], 0
+    for j in range(n):
+        src = cores[j]
+        dsts = [cores[r] for r in range(j + 1, min(n, j + WB + 1))]
+        far = [d for d in dsts if topo.rack(topo.host(d)) != topo.rack(topo.host(src))]
+        near = [d for d in dsts if d not in far]
+        if len(far) >= RELAY_MIN:
+            cand = [c for c in range(world)
+                    if topo.host(c) == topo.host(far[0]) and topo.chip(c) == topo.chip(src) and c not in cores
+                    and (topo.die(c) == topo.die(src)) == (nrel % 2 == 0)
+                    and topo.may_write(src, c) and all(topo.may_write(c, d) for d in far)]
+            plan.append(([cand[0]] + near, cand[0], far))
+            nrel += 1
+        else:
+            plan.append((far + near, None, []))
+    return plan
+
+
+def _write(g, T, topo, core, dsts, c0, c1, sem):
+    m = topo.mask(core, dsts[0])
+    for d in dsts:
+        m &= topo.mask(core, d)
+    m = _engines(m, NENG)
+    ids = []
+    for d in dsts:
+        rid, pid = topo.addr(d, core)
+        ids.append(DstId(rid=rid, pnc=pid))
+    tr = RemoteDMATransfer(dst_ids=ids, dma_engine_mask=m, remote_sem=sem, srcs=[T.kv[:, c0:c1]],
+                           dsts=[T.kv[:, c0:c1] for _ in dsts], alu_op=0)
+    g.remote_dma_fused([tr], local_sem=T.sem.snd)
+    return NENG
+
+
+def _send_block(g, T, topo, core, dsts, s, waits):
+    n = 0
+    a = s * SW
+    if SPLIT:
+        g.wait_ge(waits[0][0], waits[0][1])
+        n += _write(g, T, topo, core, dsts, a, a + 128, T.sem["ks%d" % s])
+        g.wait_ge(waits[1][0], waits[1][1])
+        n += _write(g, T, topo, core, dsts, a + 128, a + 256, T.sem["vs%d" % s])
+    else:
+        g.wait_ge(waits[0][0], waits[0][1])
+        g.wait_ge(waits[1][0], waits[1][1])
+        n += _write(g, T, topo, core, dsts, a, a + 256, T.sem["ks%d" % s])
+    return n
+
+
+def rank_program(g, core, T, topo):
+    plan = _plan(T, topo)
+    cores = list(T.cores)
+    rank = T.rank_of(core)
+    sem = T.sem
+    vname = "vs%d" if SPLIT else "ks%d"
+
+    if rank is None:
+        for j, (_, helper, far) in enumerate(plan):
+            if helper == core:
+                s = j % NS
+                n = _send_block(g, T, topo, core, far, s, [(sem["ks%d" % s], NENG), (sem[vname % s], NENG)])
+                g.wait_ge(sem.snd, n)
+        return
+
+    TE, V, S, Y = g.tensor, g.vector, g.scalar, g.sync
+    mult, amax, add = AluOpType.mult, AluOpType.max, AluOpType.add
+    Exp, Copy = ActivationFunctionType.Exp, ActivationFunctionType.Copy
+    tot, order = {}, []
+
+    def expect(name, n):
+        if name not in tot:
+            tot[name] = 0
+            order.append(name)
+        tot[name] += n
+
+    def inc(ins, name, n=1):
+        ins.then_inc(sem[name], n)
+        expect(name, n)
+
+    def way(j):
+        if core in plan[j][2]:
+            return 2
+        return 1 if topo.rack(topo.host(cores[j])) != topo.rack(topo.host(core)) else 0
+    blk = [rank] + sorted([j for j in range(max(0, rank - WB), rank)], key=lambda j: (way(j), rank - j))
+    nb = len(blk)
+    last = nb - 1
+
+    def kc(j):
+        return T.kv[:, (j % NS) * SW:(j % NS) * SW + 128]
+
+    def vc(j, extra=0):
+        return T.kv[:, (j % NS) * SW + 128:(j % NS) * SW + 256 + extra]
+
+    def tile(buf, t, off=0):
+        return buf[:, off + t * 128:off + (t + 1) * 128]
+
+    def mcol(b, t):
+        c = (b * 2 + t) * 128 + 127
+        return T.scr[:, c:c + 1]
+
+    SB = [T.ps0, T.ps1, T.ps2, T.ps3]
+    SA = [T.ps4, T.ps5]
+    L = [T.ps6, T.ps7]
+    OE = [T.ps0[:, 0:129], T.ps0[:, 256:385]]
+    O = [T.ps4[:, 256:384], T.ps5[:, 256:384]]
+
+    inc(Y.dma_start(kc(rank), T.k[:, :]), "kld", 16)
+    inc(S.dma_start(vc(rank), T.v[:, :]), "vld", 16)
+    inc(Y.dma_start(T.qs[:, :], T.q[:, :]), "qld", 16)
+
+    inc(V.memset(T.ones[:, :], 1.0), "m1")
+    inc(V.memset(T.zero[:, :], 0.0), "m3")
+    o1 = (rank % NS) * SW + 256
+    inc(V.memset(T.kv[:, o1:o1 + 8], 1.0), "m2")
+    g.wait_ge(sem.m1, 1)
+    inc(g.affine_select(T.ident[:, :], T.ones[:, :], [[-1, 128]], AluOpType.is_equal, 0.0, 0, 1), "idn")
+
+    dsts = plan[rank][0]
+    if dsts:
+        expect("snd", _send_block(g, T, topo, core, dsts, rank % NS, [(sem.kld, 16), (sem.vld, 16)]))
+    for j in blk[1:]:
+        expect("ks%d" % (j % NS), NENG)
+        if SPLIT:
+            expect("vs%d" % (j % NS), NENG)
+
+    V.wait_ge(sem.qld, 16)
+    for t in range(2):
+        inc(V.tensor_copy(tile(T.qd, t), T.qs[:, t::2]), "vq")
+
+    TE.wait_ge(sem.kld, 16)
+    TE.wait_ge(sem.vq, 2)
+    V.wait_ge(sem.m3, 1)
+    for b, j in enumerate(blk):
+        if b > 0:
+            TE.wait_ge(sem["ks%d" % (j % NS)], NENG)
+        for t in range(2):
+            if b > 0:
+                TE.wait_ge(sem["sc%d%d" % (b - 1, t)], 1)
+            inc(TE.matmul(SA[t][:, 0:128], tile(T.qd, t), kc(j), True, True), "sa%d%d" % (b, t))
+            V.wait_ge(sem["sa%d%d" % (b, t)], 1)
+            if b > 0:
+                V.wait_ge(sem["sc%d%d" % (b - 1, t)], 1)
+            c = (b * 2 + t) * 128
+            inc(V.tensor_tensor_scan(T.scr[:, c:c + 128], SA[t][:, 0:128], T.zero[:, :],
+                                     mcol(b - 1, t) if b > 0 else -1.0e29, amax, add), "sc%d%d" % (b, t))
+        TE.matmul(SB[b][:, 0:256], kc(j), T.qd[:, :], True, False)
+        if b == 0:
+            V.wait_ge(sem.idn, 1)
+            for t in range(2):
+                V.wait_ge(sem["sc0%d" % t], 1)
+                inc(V.tensor_scalar(tile(T.dg, t), T.ident[:, :], mcol(0, t), -1.0, mult, mult), "de")
+            TE.wait_ge(sem.de, 2)
+            TE.wait_ge(sem.m1, 1)
+            inc(TE.matmul(SB[0][:, 0:256], T.ones[:, :], T.dg[:, 0:256], False, True), "sb0")
+            S.wait_ge(sem.sb0, 1)
+            inc(S.activation(T.pw[:, 0:256], SB[0][:, 0:256], Exp), "p0")
+
+    for t in range(2):
+        V.wait_ge(sem["sc%d%d" % (last, t)], 1)
+        S.wait_ge(sem["sc%d%d" % (last, t)], 1)
+    if nb > 1:
+        for t in range(2):
+            inc(V.tensor_scalar(tile(T.dg, t, 256), T.ident[:, :], mcol(last, t), -1.0, mult, mult), "dd")
+    for t in range(2):
+        inc(S.activation(T.ce[:, t:t + 1], mcol(last, t), Exp, bias=mcol(0, t), scale=-1.0), "ce")
+
+    TE.wait_ge(sem.p0, 1)
+    TE.wait_ge(sem.vld, 16)
+    TE.wait_ge(sem.m2, 1)
+    for t in range(2):
+        inc(TE.matmul(OE[t], tile(T.pw, t), vc(rank, 1), True, True), "oe")
+    V.wait_ge(sem.ce, 2)
+    V.wait_ge(sem.oe, 2)
+    for t in range(2):
+        inc(V.tensor_scalar(T.ze[:, t * 136:t * 136 + 129], OE[t], T.ce[:, t:t + 1], None, mult), "ze")
+
+    if nb > 1:
+        TE.wait_ge(sem.dd, 2)
+        for b in range(1, nb):
+            inc(TE.matmul(SB[b][:, 0:256], T.ones[:, :], T.dg[:, 256:512], False, True), "sb%d" % b)
+            S.wait_ge(sem["sb%d" % b], 1)
+            inc(S.activation(T.pw[:, b * 256:(b + 1) * 256], SB[b][:, 0:256], Exp), "p%d" % b)
+
+    TE.wait_ge(sem.ze, 2)
+    TE.wait_ge(sem.idn, 1)
+    for t in range(2):
+        TE.wait_ge(sem["sc%d%d" % (last, t)], 1)
+    for t in range(2):
+        ins = TE.matmul(L[t][:, 0:1], T.ident[:, :], T.ze[:, t * 136 + 128:t * 136 + 129], True, nb == 1)
+        if nb == 1:
+            inc(ins, "ls")
+    for t in range(2):
+        ins = TE.matmul(O[t], T.ident[:, :], T.ze[:, t * 136:t * 136 + 128], True, nb == 1)
+        if nb == 1:
+            inc(ins, "os%d" % t)
+
+    def pv(b):
+        for t in range(2):
+            ins = TE.matmul(O[t], tile(T.pw, t, b * 256), vc(blk[b]), False, b == last)
+            if b == last:
+                inc(ins, "os%d" % t)
+
+    for b in range(1, nb):
+        TE.wait_ge(sem["p%d" % b], 1)
+        for t in range(2):
+            ins = TE.matmul(L[t][:, 0:1], tile(T.pw, t, b * 256), T.ones[:, 0:1], False, b == last)
+            if b == last:
+                inc(ins, "ls")
+        if not SPLIT:
+            pv(b)
+    if SPLIT:
+        for b in range(1, nb):
+            TE.wait_ge(sem["vs%d" % (blk[b] % NS)], NENG)
+            pv(b)
+
+    V.wait_ge(sem.ls, 2)
+    for t in range(2):
+        inc(V.reciprocal(T.rec[:, t:t + 1], L[t][:, 0:1]), "rc")
+    V.wait_ge(sem.rc, 2)
+    S.wait_ge(sem.rc, 2)
+    V.wait_ge(sem.os0, 1)
+    inc(V.tensor_scalar(tile(T.ysb, 0), O[0], T.rec[:, 0:1], None, mult), "ys")
+    S.wait_ge(sem.os1, 1)
+    inc(S.activation(tile(T.ysb, 1), O[1], Copy, scale=T.rec[:, 1:2]), "ys")
+    Y.wait_ge(sem.ys, 2)
+    inc(Y.dma_start(T.y[:, :], T.ysb[:, :]), "st", 16)
+
+    for name in order:
+        g.wait_ge(sem[name], tot[name])

@@ -7,9 +7,10 @@ SW = 264
 SPLIT = True
 RELAY_MIN = 2
 NENG = 8
+NCAB = 4
 
 SCRATCH = {
-    "kv": ("sbuf", [128, NS * SW], "bfloat16"),
+    "kv": ("sbuf", [128, (NS + 1) * SW], "bfloat16"),
     "qs": ("sbuf", [128, 256], "bfloat16"),
     "qd": ("sbuf", [128, 256], "bfloat16"),
     "ones": ("sbuf", [128, 128], "bfloat16"),
@@ -48,7 +49,7 @@ def _plan(T, topo):
     cores = list(T.cores)
     n = len(cores)
     world = (max(topo.host(c) for c in cores) + 1) * topo.CORES_PER_HOST
-    plan, nrel = [], 0
+    plan = []
     for j in range(n):
         src = cores[j]
         dsts = [cores[r] for r in range(j + 1, min(n, j + WB + 1))]
@@ -56,44 +57,60 @@ def _plan(T, topo):
         near = [d for d in dsts if d not in far]
         if len(far) >= RELAY_MIN:
             cand = [c for c in range(world)
-                    if topo.host(c) == topo.host(far[0]) and topo.chip(c) == topo.chip(src) and c not in cores
-                    and (topo.die(c) == topo.die(src)) == (nrel % 2 == 0)
+                    if topo.host(c) == topo.host(far[0]) and topo.chip(c) == topo.chip(src) and c not in far
                     and topo.may_write(src, c) and all(topo.may_write(c, d) for d in far)]
+            cand = [c for c in cand if c in cores] + cand
             plan.append(([cand[0]] + near, cand[0], far))
-            nrel += 1
         else:
             plan.append((far + near, None, []))
     return plan
 
 
-def _write(g, T, topo, core, dsts, c0, c1, sem):
+def _neng(entry):
+    return NCAB if len(entry[0]) == 1 and entry[1] is not None else NENG
+
+
+def _write(g, T, topo, core, dsts, src0, dst0, width, sem, neng):
     m = topo.mask(core, dsts[0])
     for d in dsts:
         m &= topo.mask(core, d)
-    m = _engines(m, NENG)
+    m = _engines(m, neng)
     ids = []
     for d in dsts:
         rid, pid = topo.addr(d, core)
         ids.append(DstId(rid=rid, pnc=pid))
-    tr = RemoteDMATransfer(dst_ids=ids, dma_engine_mask=m, remote_sem=sem, srcs=[T.kv[:, c0:c1]],
-                           dsts=[T.kv[:, c0:c1] for _ in dsts], alu_op=0)
+    tr = RemoteDMATransfer(dst_ids=ids, dma_engine_mask=m, remote_sem=sem, srcs=[T.kv[:, src0:src0 + width]],
+                           dsts=[T.kv[:, c:c + width] for c in dst0], alu_op=0)
     g.remote_dma_fused([tr], local_sem=T.sem.snd)
-    return NENG
+    return neng
 
 
-def _send_block(g, T, topo, core, dsts, s, waits):
+def _send_block(g, T, topo, core, dsts, s, src_slot, dst_slots, waits, neng):
     n = 0
-    a = s * SW
+    a = src_slot * SW
+    d0 = [x * SW for x in dst_slots]
     if SPLIT:
         g.wait_ge(waits[0][0], waits[0][1])
-        n += _write(g, T, topo, core, dsts, a, a + 128, T.sem["ks%d" % s])
+        n += _write(g, T, topo, core, dsts, a, d0, 128, T.sem["ks%d" % s], neng)
         g.wait_ge(waits[1][0], waits[1][1])
-        n += _write(g, T, topo, core, dsts, a + 128, a + 256, T.sem["vs%d" % s])
+        n += _write(g, T, topo, core, dsts, a + 128, [x + 128 for x in d0], 128, T.sem["vs%d" % s], neng)
     else:
         g.wait_ge(waits[0][0], waits[0][1])
         g.wait_ge(waits[1][0], waits[1][1])
-        n += _write(g, T, topo, core, dsts, a, a + 256, T.sem["ks%d" % s])
+        n += _write(g, T, topo, core, dsts, a, d0, 256, T.sem["ks%d" % s], neng)
     return n
+
+
+def _pass_on(g, T, topo, core, plan):
+    got = []
+    vname = "vs%d" if SPLIT else "ks%d"
+    for j, entry in enumerate(plan):
+        if entry[1] == core:
+            s, ne = j % NS, _neng(entry)
+            n = _send_block(g, T, topo, core, entry[2], s, NS, [s for _ in entry[2]],
+                            [(T.sem["ks%d" % s], ne), (T.sem[vname % s], ne)], NENG)
+            got += [("ks%d" % s, ne), ("snd", n)] + ([("vs%d" % s, ne)] if SPLIT else [])
+    return got
 
 
 def rank_program(g, core, T, topo):
@@ -101,13 +118,10 @@ def rank_program(g, core, T, topo):
     cores = list(T.cores)
     rank = T.rank_of(core)
     sem = T.sem
-    vname = "vs%d" if SPLIT else "ks%d"
 
     if rank is None:
-        for j, (_, helper, far) in enumerate(plan):
-            if helper == core:
-                s = j % NS
-                n = _send_block(g, T, topo, core, far, s, [(sem["ks%d" % s], NENG), (sem[vname % s], NENG)])
+        for name, n in _pass_on(g, T, topo, core, plan):
+            if name == "snd":
                 g.wait_ge(sem.snd, n)
         return
 
@@ -166,11 +180,17 @@ def rank_program(g, core, T, topo):
 
     dsts = plan[rank][0]
     if dsts:
-        expect("snd", _send_block(g, T, topo, core, dsts, rank % NS, [(sem.kld, 16), (sem.vld, 16)]))
+        expect("snd", _send_block(g, T, topo, core, dsts, rank % NS, rank % NS,
+                                  [NS if d == plan[rank][1] else rank % NS for d in dsts],
+                                  [(sem.kld, 16), (sem.vld, 16)], _neng(plan[rank])))
+    for name, n in _pass_on(g, T, topo, core, plan):
+        expect(name, n)
+    cnt = {}
     for j in blk[1:]:
-        expect("ks%d" % (j % NS), NENG)
+        cnt[j] = NENG if core in plan[j][2] else _neng(plan[j])
+        expect("ks%d" % (j % NS), cnt[j])
         if SPLIT:
-            expect("vs%d" % (j % NS), NENG)
+            expect("vs%d" % (j % NS), cnt[j])
 
     V.wait_ge(sem.qld, 16)
     for t in range(2):
@@ -181,7 +201,7 @@ def rank_program(g, core, T, topo):
     V.wait_ge(sem.m3, 1)
     for b, j in enumerate(blk):
         if b > 0:
-            TE.wait_ge(sem["ks%d" % (j % NS)], NENG)
+            TE.wait_ge(sem["ks%d" % (j % NS)], cnt[j])
         for t in range(2):
             if b > 0:
                 TE.wait_ge(sem["sc%d%d" % (b - 1, t)], 1)
@@ -259,7 +279,7 @@ def rank_program(g, core, T, topo):
             pv(b)
     if SPLIT:
         for b in range(1, nb):
-            TE.wait_ge(sem["vs%d" % (blk[b] % NS)], NENG)
+            TE.wait_ge(sem["vs%d" % (blk[b] % NS)], cnt[blk[b]])
             pv(b)
 
     V.wait_ge(sem.ls, 2)

from concourse.bass import DstId, RemoteDMATransfer
from concourse.mybir import AluOpType, ActivationFunctionType

WB = 3
NS = WB + 1
SW = 264
SPLIT = True
RELAY_MIN = 2
NENG = 8
NCAB = 4

SCRATCH = {
    "kv": ("sbuf", [128, (NS + 1) * SW], "bfloat16"),
    "qs": ("sbuf", [128, 256], "bfloat16"),
    "qd": ("sbuf", [128, 256], "bfloat16"),
    "ones": ("sbuf", [128, 128], "bfloat16"),
    "zero": ("sbuf", [128, 128], "bfloat16"),
    "ident": ("sbuf", [128, 128], "bfloat16"),
    "scr": ("sbuf", [128, 2 * NS * 128], "bfloat16"),
    "dg": ("sbuf", [128, 512], "bfloat16"),
    "pw": ("sbuf", [128, NS * 256], "bfloat16"),
    "ze": ("sbuf", [128, 2 * 136], "bfloat16"),
    "ce": ("sbuf", [128, 4], "float32"),
    "rec": ("sbuf", [128, 4], "float32"),
    "ysb": ("sbuf", [128, 256], "bfloat16"),
}
for _i in range(8):
    SCRATCH["ps%d" % _i] = ("psum", [128, 512], "float32")

SEMAPHORES = (["kld", "vld", "qld", "m1", "m2", "m3", "idn", "vq", "de", "dd", "oe", "ce", "ze", "ls", "rc",
               "os0", "os1", "ys", "st", "snd"]
              + ["ks%d" % s for s in range(NS)] + ["vs%d" % s for s in range(NS)]
              + ["sa%d%d" % (b, t) for b in range(NS) for t in range(2)]
              + ["sc%d%d" % (b, t) for b in range(NS) for t in range(2)]
              + ["sb%d" % b for b in range(NS)] + ["p%d" % b for b in range(NS)])


def _engines(mask, n):
    out, c, b = 0, 0, 1
    while c < n:
        if mask & b:
            out |= b
            c += 1
        b <<= 1
    return out


def _plan(T, topo):
    cores = list(T.cores)
    n = len(cores)
    world = (max(topo.host(c) for c in cores) + 1) * topo.CORES_PER_HOST
    plan = []
    for j in range(n):
        src = cores[j]
        dsts = [cores[r] for r in range(j + 1, min(n, j + WB + 1))]
        far = [d for d in dsts if topo.rack(topo.host(d)) != topo.rack(topo.host(src))]
        near = [d for d in dsts if d not in far]
        if len(far) >= RELAY_MIN:
            cand = [c for c in range(world)
                    if topo.host(c) == topo.host(far[0]) and topo.chip(c) == topo.chip(src) and c not in far
                    and topo.may_write(src, c) and all(topo.may_write(c, d) for d in far)]
            cand = [c for c in cand if c in cores] + cand
            plan.append(([cand[0]] + near, cand[0], far))
        else:
            plan.append((far + near, None, []))
    return plan


def _neng(entry):
    return NCAB if len(entry[0]) == 1 and entry[1] is not None else NENG


def _write(g, T, topo, core, dsts, src0, dst0, width, sem, neng):
    m = topo.mask(core, dsts[0])
    for d in dsts:
        m &= topo.mask(core, d)
    m = _engines(m, neng)
    ids = []
    for d in dsts:
        rid, pid = topo.addr(d, core)
        ids.append(DstId(rid=rid, pnc=pid))
    tr = RemoteDMATransfer(dst_ids=ids, dma_engine_mask=m, remote_sem=sem, srcs=[T.kv[:, src0:src0 + width]],
                           dsts=[T.kv[:, c:c + width] for c in dst0], alu_op=0)
    g.remote_dma_fused([tr], local_sem=T.sem.snd)
    return neng


def _send_block(g, T, topo, core, dsts, s, src_slot, dst_slots, waits, neng):
    n = 0
    a = src_slot * SW
    d0 = [x * SW for x in dst_slots]
    if SPLIT:
        g.wait_ge(waits[0][0], waits[0][1])
        n += _write(g, T, topo, core, dsts, a, d0, 128, T.sem["ks%d" % s], neng)
        g.wait_ge(waits[1][0], waits[1][1])
        n += _write(g, T, topo, core, dsts, a + 128, [x + 128 for x in d0], 128, T.sem["vs%d" % s], neng)
    else:
        g.wait_ge(waits[0][0], waits[0][1])
        g.wait_ge(waits[1][0], waits[1][1])
        n += _write(g, T, topo, core, dsts, a, d0, 256, T.sem["ks%d" % s], neng)
    return n


def _pass_on(g, T, topo, core, plan):
    got = []
    vname = "vs%d" if SPLIT else "ks%d"
    for j, entry in enumerate(plan):
        if entry[1] == core:
            s, ne = j % NS, _neng(entry)
            n = _send_block(g, T, topo, core, entry[2], s, NS, [s for _ in entry[2]],
                            [(T.sem["ks%d" % s], ne), (T.sem[vname % s], ne)], NENG)
            got += [("ks%d" % s, ne), ("snd", n)] + ([("vs%d" % s, ne)] if SPLIT else [])
    return got


def rank_program(g, core, T, topo):
    plan = _plan(T, topo)
    cores = list(T.cores)
    rank = T.rank_of(core)
    sem = T.sem

    if rank is None:
        for name, n in _pass_on(g, T, topo, core, plan):
            if name == "snd":
                g.wait_ge(sem.snd, n)
        return

    TE, V, S, Y = g.tensor, g.vector, g.scalar, g.sync
    mult, amax, add = AluOpType.mult, AluOpType.max, AluOpType.add
    Exp, Copy = ActivationFunctionType.Exp, ActivationFunctionType.Copy
    tot, order = {}, []

    def expect(name, n):
        if name not in tot:
            tot[name] = 0
            order.append(name)
        tot[name] += n

    def inc(ins, name, n=1):
        ins.then_inc(sem[name], n)
        expect(name, n)

    def way(j):
        if core in plan[j][2]:
            return 2
        return 1 if topo.rack(topo.host(cores[j])) != topo.rack(topo.host(core)) else 0
    blk = [rank] + sorted([j for j in range(max(0, rank - WB), rank)], key=lambda j: (way(j), rank - j))
    nb = len(blk)
    last = nb - 1

    def kc(j):
        return T.kv[:, (j % NS) * SW:(j % NS) * SW + 128]

    def vc(j, extra=0):
        return T.kv[:, (j % NS) * SW + 128:(j % NS) * SW + 256 + extra]

    def tile(buf, t, off=0):
        return buf[:, off + t * 128:off + (t + 1) * 128]

    def mcol(b, t):
        c = (b * 2 + t) * 128 + 127
        return T.scr[:, c:c + 1]

    SB = [T.ps0, T.ps1, T.ps2, T.ps3]
    SA = [T.ps4, T.ps5]
    L = [T.ps6, T.ps7]
    OE = [T.ps0[:, 0:129], T.ps0[:, 256:385]]
    O = [T.ps4[:, 256:384], T.ps5[:, 256:384]]

    inc(Y.dma_start(kc(rank), T.k[:, :]), "kld", 16)
    inc(S.dma_start(vc(rank), T.v[:, :]), "vld", 16)
    inc(Y.dma_start(T.qs[:, :], T.q[:, :]), "qld", 16)

    inc(V.memset(T.ones[:, :], 1.0), "m1")
    inc(V.memset(T.zero[:, :], 0.0), "m3")
    o1 = (rank % NS) * SW + 256
    inc(V.memset(T.kv[:, o1:o1 + 8], 1.0), "m2")
    g.wait_ge(sem.m1, 1)
    inc(g.affine_select(T.ident[:, :], T.ones[:, :], [[-1, 128]], AluOpType.is_equal, 0.0, 0, 1), "idn")

    dsts = plan[rank][0]
    if dsts:
        expect("snd", _send_block(g, T, topo, core, dsts, rank % NS, rank % NS,
                                  [NS if d == plan[rank][1] else rank % NS for d in dsts],
                                  [(sem.kld, 16), (sem.vld, 16)], _neng(plan[rank])))
    for name, n in _pass_on(g, T, topo, core, plan):
        expect(name, n)
    cnt = {}
    for j in blk[1:]:
        cnt[j] = NENG if core in plan[j][2] else _neng(plan[j])
        expect("ks%d" % (j % NS), cnt[j])
        if SPLIT:
            expect("vs%d" % (j % NS), cnt[j])

    V.wait_ge(sem.qld, 16)
    for t in range(2):
        inc(V.tensor_copy(tile(T.qd, t), T.qs[:, t::2]), "vq")

    TE.wait_ge(sem.kld, 16)
    TE.wait_ge(sem.vq, 2)
    V.wait_ge(sem.m3, 1)
    for b, j in enumerate(blk):
        if b > 0:
            TE.wait_ge(sem["ks%d" % (j % NS)], cnt[j])
        for t in range(2):
            if b > 0:
                TE.wait_ge(sem["sc%d%d" % (b - 1, t)], 1)
            inc(TE.matmul(SA[t][:, 0:128], tile(T.qd, t), kc(j), True, True), "sa%d%d" % (b, t))
            V.wait_ge(sem["sa%d%d" % (b, t)], 1)
            if b > 0:
                V.wait_ge(sem["sc%d%d" % (b - 1, t)], 1)
            c = (b * 2 + t) * 128
            inc(V.tensor_tensor_scan(T.scr[:, c:c + 128], SA[t][:, 0:128], T.zero[:, :],
                                     mcol(b - 1, t) if b > 0 else -1.0e29, amax, add), "sc%d%d" % (b, t))
        TE.matmul(SB[b][:, 0:256], kc(j), T.qd[:, :], True, False)
        if b == 0:
            V.wait_ge(sem.idn, 1)
            for t in range(2):
                V.wait_ge(sem["sc0%d" % t], 1)
                inc(V.tensor_scalar(tile(T.dg, t), T.ident[:, :], mcol(0, t), -1.0, mult, mult), "de")
            TE.wait_ge(sem.de, 2)
            TE.wait_ge(sem.m1, 1)
            inc(TE.matmul(SB[0][:, 0:256], T.ones[:, :], T.dg[:, 0:256], False, True), "sb0")
            S.wait_ge(sem.sb0, 1)
            inc(S.activation(T.pw[:, 0:256], SB[0][:, 0:256], Exp), "p0")

    for t in range(2):
        V.wait_ge(sem["sc%d%d" % (last, t)], 1)
        S.wait_ge(sem["sc%d%d" % (last, t)], 1)
    if nb > 1:
        for t in range(2):
            inc(V.tensor_scalar(tile(T.dg, t, 256), T.ident[:, :], mcol(last, t), -1.0, mult, mult), "dd")
    for t in range(2):
        inc(S.activation(T.ce[:, t:t + 1], mcol(last, t), Exp, bias=mcol(0, t), scale=-1.0), "ce")

    TE.wait_ge(sem.p0, 1)
    TE.wait_ge(sem.vld, 16)
    TE.wait_ge(sem.m2, 1)
    for t in range(2):
        inc(TE.matmul(OE[t], tile(T.pw, t), vc(rank, 1), True, True), "oe")
    V.wait_ge(sem.ce, 2)
    V.wait_ge(sem.oe, 2)
    for t in range(2):
        inc(V.tensor_scalar(T.ze[:, t * 136:t * 136 + 129], OE[t], T.ce[:, t:t + 1], None, mult), "ze")

    if nb > 1:
        TE.wait_ge(sem.dd, 2)
        for b in range(1, nb):
            inc(TE.matmul(SB[b][:, 0:256], T.ones[:, :], T.dg[:, 256:512], False, True), "sb%d" % b)
            S.wait_ge(sem["sb%d" % b], 1)
            inc(S.activation(T.pw[:, b * 256:(b + 1) * 256], SB[b][:, 0:256], Exp), "p%d" % b)

    TE.wait_ge(sem.ze, 2)
    TE.wait_ge(sem.idn, 1)
    for t in range(2):
        TE.wait_ge(sem["sc%d%d" % (last, t)], 1)
    for t in range(2):
        ins = TE.matmul(L[t][:, 0:1], T.ident[:, :], T.ze[:, t * 136 + 128:t * 136 + 129], True, nb == 1)
        if nb == 1:
            inc(ins, "ls")
    for t in range(2):
        ins = TE.matmul(O[t], T.ident[:, :], T.ze[:, t * 136:t * 136 + 128], True, nb == 1)
        if nb == 1:
            inc(ins, "os%d" % t)

    def pv(b):
        for t in range(2):
            ins = TE.matmul(O[t], tile(T.pw, t, b * 256), vc(blk[b]), False, b == last)
            if b == last:
                inc(ins, "os%d" % t)

    for b in range(1, nb):
        TE.wait_ge(sem["p%d" % b], 1)
        for t in range(2):
            ins = TE.matmul(L[t][:, 0:1], tile(T.pw, t, b * 256), T.ones[:, 0:1], False, b == last)
            if b == last:
                inc(ins, "ls")
        if not SPLIT:
            pv(b)
    if SPLIT:
        for b in range(1, nb):
            TE.wait_ge(sem["vs%d" % (blk[b] % NS)], cnt[blk[b]])
            pv(b)

    V.wait_ge(sem.ls, 2)
    for t in range(2):
        inc(V.reciprocal(T.rec[:, t:t + 1], L[t][:, 0:1]), "rc")
    V.wait_ge(sem.rc, 2)
    S.wait_ge(sem.rc, 2)
    V.wait_ge(sem.os0, 1)
    inc(V.tensor_scalar(tile(T.ysb, 0), O[0], T.rec[:, 0:1], None, mult), "ys")
    S.wait_ge(sem.os1, 1)
    inc(S.activation(tile(T.ysb, 1), O[1], Copy, scale=T.rec[:, 1:2]), "ys")
    Y.wait_ge(sem.ys, 2)
    inc(Y.dma_start(T.y[:, :], T.ysb[:, :]), "st", 16)

    for name in order:
        g.wait_ge(sem[name], tot[name])
